import numpy as np
CORES = [8,136,40,168]
N = 4
F = 128
BOUND = 4579.5
def setup_inputs(rng):
    gr = rng.standard_normal((1, 128, N * F), dtype=np.float32) + rng.standard_normal((N, 128, N * F), dtype=np.float32)
    return {"gr": gr}
def setup_inputs_big(rng):
    d = setup_inputs(rng)
    for k in ("gr",): d[k] = (d[k].astype(np.float32) * 1024.0).astype(d[k].dtype)
    return d
def setup_inputs_small(rng):
    d = setup_inputs(rng)
    for k in ("gr",): d[k] = (d[k].astype(np.float32) * (1 / 1024.0)).astype(d[k].dtype)
    return d
def setup_inputs_apart(rng):
    d = setup_inputs(rng)
    f = (10.0 ** rng.permutation(np.linspace(-1.5, 1.5, N))).astype(np.float32).reshape(N, 1, 1)
    for k in ("gr",): d[k] = (d[k].astype(np.float32) * f).astype(d[k].dtype)
    return d
def setup_inputs_far(rng):
    d = setup_inputs(rng)
    for k in ("gr",): d[k] = (d[k].astype(np.float32) * 16384.0).astype(d[k].dtype)
    return d
def setup_inputs_over(rng):
    d = setup_inputs(rng)
    f = np.float32(10.0 ** rng.uniform(1.5, 3.5)) * np.where(rng.random((1, 128, N * F)) < 0.5, 0.1, 1.0).astype(np.float32)
    for k in ("gr",): d[k] = (d[k].astype(np.float32) * f).astype(d[k].dtype)
    return d
def reference(gr):
    s = gr.astype(np.float64).sum(axis=0)
    nrm = np.sqrt((s ** 2).sum())
    s = s * min(1.0, BOUND / nrm)
    return {"y": np.stack([s[:, F * r:F * r + F] for r in range(N)]).astype(np.float32)}

@@ -1,0 +1,103 @@
+from concourse.bass import DstId, RemoteDMATransfer
+from concourse.mybir import AluOpType, ActivationFunctionType
+
+N = 4
+F = 128
+
+SCRATCH = {
+    "snd": ("sbuf", [128, (N - 1) * F], "float32"),
+    "own": ("sbuf", [128, F], "float32"),
+    "land": ("sbuf", [128, (N - 1) * F], "float32"),
+    "ones": ("sbuf", [128, 128], "float32"),
+    "qall": ("sbuf", [128, 8], "float32"),
+    "cst": ("sbuf", [128, 8], "float32"),
+    "scn": ("sbuf", [128, 8], "float32"),
+    "sm": ("sbuf", [128, 4], "float32"),
+    "yo": ("sbuf", [128, F], "float32"),
+    "acc": ("psum", [128, 512], "float32"),
+    "tot": ("psum", [128, 512], "float32"),
+}
+SEMAPHORES = ["ld1", "ld2", "ld3", "ldo", "arr1", "arr2", "arr3", "qarr", "sent",
+              "fill", "added", "squared", "summed", "scanned", "rooted", "inverted", "scaled", "stored"]
+
+
+def rank_program(g, core, T, topo):
+    r = T.rank_of(core)
+    if r is None:
+        return
+    S = T.sem
+    add, mult, vmax = AluOpType.add, AluOpType.mult, AluOpType.max
+    bound = float(T.tables["BOUND"])
+    peers = [T.cores[(r + k) % N] for k in range(1, N)]
+    masks = [topo.mask(core, d) for d in peers]
+    common = masks[0] & masks[1] & masks[2]
+    eng = [bin(m).count("1") for m in masks]
+    ceng = bin(common).count("1")
+    eng_in = [bin(topo.mask(T.cores[(r - k) % N], core)).count("1") for k in range(1, N)]
+    ceng_in = 0
+    for k in range(1, N):
+        src = T.cores[(r - k) % N]
+        m = 0xFFFF
+        for j in range(1, N):
+            m &= topo.mask(src, T.cores[(r - k + j) % N])
+        ceng_in += bin(m).count("1")
+
+    for k in range(1, N):
+        b = (r + k) % N
+        g.sync.dma_start(T.snd[:, (k - 1) * F:k * F], T.gr[:, b * F:(b + 1) * F]).then_inc(S["ld%d" % k], 16)
+    g.sync.dma_start(T.own[:], T.gr[:, r * F:(r + 1) * F]).then_inc(S.ldo, 16)
+
+    for k in range(1, N):
+        rid, pid = topo.addr(peers[k - 1], core)
+        g.wait_ge(S["ld%d" % k], 16)
+        g.remote_dma(T.land[:, (k - 1) * F:k * F], T.snd[:, (k - 1) * F:k * F], S["arr%d" % k], S.sent,
+                     pid, rid, masks[k - 1])
+    ids = []
+    for d in peers:
+        rid, pid = topo.addr(d, core)
+        ids.append(DstId(rid=rid, pnc=pid))
+    g.wait_ge(S.squared, 1)
+    g.remote_dma_fused([RemoteDMATransfer(dst_ids=ids, dma_engine_mask=common, remote_sem=S.qarr,
+                                          srcs=[T.qall[:, 0:1]],
+                                          dsts=[T.qall[:, 3 + k:4 + k] for k in range(1, N)])],
+                       local_sem=S.sent)
+    g.wait_ge(S.sent, sum(eng) + ceng)
+
+    v = g.vector
+    v.memset(T.ones[:], 1.0).then_inc(S.fill, 1)
+    v.memset(T.qall[:, 1:4], 0.0).then_inc(S.fill, 1)
+    v.memset(T.cst[:, 0:6], 0.0).then_inc(S.fill, 1)
+    v.memset(T.cst[:, 6:7], 1.0).then_inc(S.fill, 1)
+    acc = T.acc[:, 0:F]
+    v.wait_ge(S.ldo, 16)
+    v.wait_ge(S.arr1, eng_in[0])
+    v.tensor_tensor(acc, T.own[:], T.land[:, 0:F], add).then_inc(S.added, 1)
+    for k in range(2, N):
+        v.wait_ge(S["arr%d" % k], eng_in[k - 1])
+        v.wait_ge(S.added, k - 1)
+        v.tensor_tensor(acc, acc, T.land[:, (k - 1) * F:k * F], add).then_inc(S.added, 1)
+    v.wait_ge(S.added, N - 1)
+    v.wait_ge(S.fill, 4)
+    v.wait_ge(S.summed, 1)
+    v.tensor_tensor_scan(T.scn[:, 0:7], T.tot[:, 0:7], T.cst[:, 0:7], 0.0, add, vmax).then_inc(S.scanned, 1)
+    v.wait_ge(S.rooted, 1)
+    v.reciprocal(T.sm[:, 1:2], T.sm[:, 0:1]).then_inc(S.inverted, 1)
+    v.wait_ge(S.inverted, 1)
+    v.tensor_scalar(T.yo[:], acc, T.sm[:, 1:2], 2.0 ** -25, mult, mult).then_inc(S.scaled, 1)
+
+    a = g.scalar
+    a.wait_ge(S.added, N - 1)
+    a.activation(T.yo[:], acc, ActivationFunctionType.Square, scale=1.0 / bound,
+                 accum_out=T.qall[:, 0:1]).then_inc(S.squared, 1)
+    a.wait_ge(S.scanned, 1)
+    a.activation(T.sm[:, 0:1], T.scn[:, 6:7], ActivationFunctionType.Sqrt, scale=2.0 ** -50).then_inc(S.rooted, 1)
+
+    p = g.tensor
+    p.wait_ge(S.fill, 4)
+    p.wait_ge(S.squared, 1)
+    p.wait_ge(S.qarr, ceng_in)
+    p.matmul(T.tot[:, 0:7], T.ones[:], T.qall[:, 0:7], True, True).then_inc(S.summed, 1)
+
+    g.sync.wait_ge(S.scaled, 1)
+    g.sync.dma_start(T.y[:], T.yo[:]).then_inc(S.stored, 16)
+    g.sync.wait_ge(S.stored, 16)

@@ -37,7 +37,7 @@ def rank_program(g, core, T, topo):
     ceng_in = 0
     for k in range(1, N):
         src = T.cores[(r - k) % N]
-        m = 0xFFFF
+        m = topo.mask(src, core)
         for j in range(1, N):
             m &= topo.mask(src, T.cores[(r - k + j) % N])
         ceng_in += bin(m).count("1")
@@ -76,21 +76,26 @@ def rank_program(g, core, T, topo):
         v.wait_ge(S["arr%d" % k], eng_in[k - 1])
         v.wait_ge(S.added, k - 1)
         v.tensor_tensor(acc, acc, T.land[:, (k - 1) * F:k * F], add).then_inc(S.added, 1)
+    q = T.scn[:, 6:7]
+    root, inv, inv2 = T.sm[:, 0:1], T.sm[:, 1:2], T.sm[:, 2:3]
     v.wait_ge(S.added, N - 1)
     v.wait_ge(S.fill, 4)
     v.wait_ge(S.summed, 1)
     v.tensor_tensor_scan(T.scn[:, 0:7], T.tot[:, 0:7], T.cst[:, 0:7], 0.0, add, vmax).then_inc(S.scanned, 1)
-    v.wait_ge(S.rooted, 1)
-    v.reciprocal(T.sm[:, 1:2], T.sm[:, 0:1]).then_inc(S.inverted, 1)
+    v.wait_ge(S.scanned, 1)
+    v.reciprocal(inv, q).then_inc(S.inverted, 1)
     v.wait_ge(S.inverted, 1)
-    v.tensor_scalar(T.yo[:], acc, T.sm[:, 1:2], 2.0 ** -25, mult, mult).then_inc(S.scaled, 1)
+    v.tensor_scalar(inv2, inv, 2.0 ** 25, None, mult).then_inc(S.inverted, 1)
+    v.wait_ge(S.inverted, 2)
+    v.wait_ge(S.rooted, 1)
+    v.tensor_scalar(T.yo[:], acc, inv2, root, mult, mult).then_inc(S.scaled, 1)
 
     a = g.scalar
     a.wait_ge(S.added, N - 1)
     a.activation(T.yo[:], acc, ActivationFunctionType.Square, scale=1.0 / bound,
                  accum_out=T.qall[:, 0:1]).then_inc(S.squared, 1)
     a.wait_ge(S.scanned, 1)
-    a.activation(T.sm[:, 0:1], T.scn[:, 6:7], ActivationFunctionType.Sqrt, scale=2.0 ** -50).then_inc(S.rooted, 1)
+    a.activation(root, q, ActivationFunctionType.Sqrt, scale=2.0 ** -50).then_inc(S.rooted, 1)
 
     p = g.tensor
     p.wait_ge(S.fill, 4)

@@ -3,6 +3,12 @@ from concourse.mybir import AluOpType, ActivationFunctionType
 
 N = 4
 F = 128
+NT = 52
+POLY = [0.632455572, 0.189735067, 0.08537769384, 0.04273377586, 0.02247123916, 0.01177503762, 0.006322641527,
+        0.004754951238, 0.002970944884, -0.000370359018, -0.0004744689166, 0.001371374271, 0.0008763282976]
+DEG = len(POLY) - 1
+NS = NT + DEG - 1
+BIG = 1.0e9
 
 SCRATCH = {
     "snd": ("sbuf", [128, (N - 1) * F], "float32"),
@@ -12,13 +18,24 @@ SCRATCH = {
     "qall": ("sbuf", [128, 8], "float32"),
     "cst": ("sbuf", [128, 8], "float32"),
     "scn": ("sbuf", [128, 8], "float32"),
-    "sm": ("sbuf", [128, 4], "float32"),
+    "mul": ("sbuf", [128, 3 * NT], "float32"),
+    "zer": ("sbuf", [128, NT], "float32"),
+    "th": ("sbuf", [128, NT], "float32"),
+    "gs": ("sbuf", [128, NT], "float32"),
+    "hn": ("sbuf", [128, NT], "float32"),
+    "cf": ("sbuf", [128, DEG], "float32"),
+    "fl": ("sbuf", [128, NS], "float32"),
+    "tt": ("sbuf", [128, NS], "float32"),
+    "ts": ("sbuf", [128, NS], "float32"),
+    "hs": ("sbuf", [128, NT], "float32"),
+    "ps": ("sbuf", [128, DEG], "float32"),
     "yo": ("sbuf", [128, F], "float32"),
     "acc": ("psum", [128, 512], "float32"),
     "tot": ("psum", [128, 512], "float32"),
 }
 SEMAPHORES = ["ld1", "ld2", "ld3", "ldo", "arr1", "arr2", "arr3", "qarr", "sent",
-              "fill", "added", "squared", "summed", "scanned", "rooted", "inverted", "scaled", "stored"]
+              "fill", "tabs", "added", "squared", "summed", "scanned", "flagged", "spread", "picked", "hpicked",
+              "horner", "scaled", "stored"]
 
 
 def rank_program(g, core, T, topo):
@@ -26,7 +43,7 @@ def rank_program(g, core, T, topo):
     if r is None:
         return
     S = T.sem
-    add, mult, vmax = AluOpType.add, AluOpType.mult, AluOpType.max
+    add, mult, vmax, is_gt = AluOpType.add, AluOpType.mult, AluOpType.max, AluOpType.is_gt
     bound = float(T.tables["BOUND"])
     peers = [T.cores[(r + k) % N] for k in range(1, N)]
     masks = [topo.mask(core, d) for d in peers]
@@ -64,10 +81,21 @@ def rank_program(g, core, T, topo):
     g.wait_ge(S.sent, sum(eng) + ceng)
 
     v = g.vector
-    v.memset(T.ones[:], 1.0).then_inc(S.fill, 1)
-    v.memset(T.qall[:, 1:4], 0.0).then_inc(S.fill, 1)
-    v.memset(T.cst[:, 0:6], 0.0).then_inc(S.fill, 1)
-    v.memset(T.cst[:, 6:7], 1.0).then_inc(S.fill, 1)
+    fills = [(T.ones[:], 1.0), (T.qall[:, 1:4], 0.0), (T.cst[:, 0:6], 0.0), (T.cst[:, 6:7], 1.0),
+             (T.zer[:], 0.0),
+             (T.mul[:, 0:1], 2.0 ** 5), (T.mul[:, 1:NT], 0.25),
+             (T.mul[:, NT:2 * NT], 4.0), (T.mul[:, 2 * NT:3 * NT], 2.0),
+             (T.fl[:, NT:NS], 0.0), (T.tt[:, NT:NS], -2.0)]
+    for j in range(DEG):
+        fills.append((T.cf[:, j:j + 1], -POLY[DEG - 1 - j]))
+    for ap, val in fills:
+        v.memset(ap, val).then_inc(S.fill, 1)
+    nfill = len(fills)
+    v.wait_ge(S.fill, nfill)
+    v.tensor_tensor_scan(T.th[:], T.mul[:, 0:NT], T.zer[:], 2.0 ** (2 * NT - 5), mult, add).then_inc(S.tabs, 1)
+    v.tensor_tensor_scan(T.gs[:], T.mul[:, NT:2 * NT], T.zer[:], -(4.0 ** -NT) / 1.5, mult, add).then_inc(S.tabs, 1)
+    v.tensor_tensor_scan(T.hn[:], T.mul[:, 2 * NT:3 * NT], T.zer[:], -(2.0 ** -NT), mult, add).then_inc(S.tabs, 1)
+
     acc = T.acc[:, 0:F]
     v.wait_ge(S.ldo, 16)
     v.wait_ge(S.arr1, eng_in[0])
@@ -76,29 +104,34 @@ def rank_program(g, core, T, topo):
         v.wait_ge(S["arr%d" % k], eng_in[k - 1])
         v.wait_ge(S.added, k - 1)
         v.tensor_tensor(acc, acc, T.land[:, (k - 1) * F:k * F], add).then_inc(S.added, 1)
+
     q = T.scn[:, 6:7]
-    root, inv, inv2 = T.sm[:, 0:1], T.sm[:, 1:2], T.sm[:, 2:3]
     v.wait_ge(S.added, N - 1)
-    v.wait_ge(S.fill, 4)
+    v.wait_ge(S.tabs, 3)
     v.wait_ge(S.summed, 1)
     v.tensor_tensor_scan(T.scn[:, 0:7], T.tot[:, 0:7], T.cst[:, 0:7], 0.0, add, vmax).then_inc(S.scanned, 1)
     v.wait_ge(S.scanned, 1)
-    v.reciprocal(inv, q).then_inc(S.inverted, 1)
-    v.wait_ge(S.inverted, 1)
-    v.tensor_scalar(inv2, inv, 2.0 ** 25, None, mult).then_inc(S.inverted, 1)
-    v.wait_ge(S.inverted, 2)
-    v.wait_ge(S.rooted, 1)
-    v.tensor_scalar(T.yo[:], acc, inv2, root, mult, mult).then_inc(S.scaled, 1)
+    v.tensor_scalar(T.fl[:, 0:NT], T.th[:], q, -BIG, is_gt, mult).then_inc(S.flagged, 1)
+    v.wait_ge(S.flagged, 1)
+    v.wait_ge(S.spread, 1)
+    v.tensor_tensor_scan(T.ts[:], T.fl[:], T.tt[:], 0.0, add, vmax).then_inc(S.picked, 1)
+    v.tensor_tensor_scan(T.hs[:], T.fl[:, 0:NT], T.hn[:], 0.0, add, vmax).then_inc(S.hpicked, 1)
+    v.wait_ge(S.picked, 1)
+    v.tensor_tensor_scan(T.ps[:], T.ts[:, NT - 1:NS], T.cf[:], -POLY[DEG], mult, add).then_inc(S.horner, 1)
+    v.wait_ge(S.horner, 1)
+    v.wait_ge(S.hpicked, 1)
+    v.tensor_scalar(T.yo[:], acc, T.hs[:, NT - 1:NT], T.ps[:, DEG - 1:DEG], mult, mult).then_inc(S.scaled, 1)
 
     a = g.scalar
     a.wait_ge(S.added, N - 1)
     a.activation(T.yo[:], acc, ActivationFunctionType.Square, scale=1.0 / bound,
                  accum_out=T.qall[:, 0:1]).then_inc(S.squared, 1)
+    a.wait_ge(S.tabs, 3)
     a.wait_ge(S.scanned, 1)
-    a.activation(root, q, ActivationFunctionType.Sqrt, scale=2.0 ** -50).then_inc(S.rooted, 1)
+    a.activation(T.tt[:, 0:NT], T.gs[:], ActivationFunctionType.Identity, bias=5.0 / 3.0, scale=q).then_inc(S.spread, 1)
 
     p = g.tensor
-    p.wait_ge(S.fill, 4)
+    p.wait_ge(S.fill, nfill)
     p.wait_ge(S.squared, 1)
     p.wait_ge(S.qarr, ceng_in)
     p.matmul(T.tot[:, 0:7], T.ones[:], T.qall[:, 0:7], True, True).then_inc(S.summed, 1)

from concourse.bass import DstId, RemoteDMATransfer
from concourse.mybir import AluOpType, ActivationFunctionType

N = 4
F = 128
NT = 52
POLY = [0.632455572, 0.189735067, 0.08537769384, 0.04273377586, 0.02247123916, 0.01177503762, 0.006322641527,
        0.004754951238, 0.002970944884, -0.000370359018, -0.0004744689166, 0.001371374271, 0.0008763282976]
DEG = len(POLY) - 1
NS = NT + DEG - 1
BIG = 1.0e9

SCRATCH = {
    "snd": ("sbuf", [128, (N - 1) * F], "float32"),
    "own": ("sbuf", [128, F], "float32"),
    "land": ("sbuf", [128, (N - 1) * F], "float32"),
    "ones": ("sbuf", [128, 128], "float32"),
    "qall": ("sbuf", [128, 8], "float32"),
    "cst": ("sbuf", [128, 8], "float32"),
    "scn": ("sbuf", [128, 8], "float32"),
    "mul": ("sbuf", [128, 3 * NT], "float32"),
    "zer": ("sbuf", [128, NT], "float32"),
    "th": ("sbuf", [128, NT], "float32"),
    "gs": ("sbuf", [128, NT], "float32"),
    "hn": ("sbuf", [128, NT], "float32"),
    "cf": ("sbuf", [128, DEG], "float32"),
    "fl": ("sbuf", [128, NS], "float32"),
    "tt": ("sbuf", [128, NS], "float32"),
    "ts": ("sbuf", [128, NS], "float32"),
    "hs": ("sbuf", [128, NT], "float32"),
    "ps": ("sbuf", [128, DEG], "float32"),
    "yo": ("sbuf", [128, F], "float32"),
    "acc": ("psum", [128, 512], "float32"),
    "tot": ("psum", [128, 512], "float32"),
}
SEMAPHORES = ["ld1", "ld2", "ld3", "ldo", "arr1", "arr2", "arr3", "qarr", "sent",
              "fill", "tabs", "added", "squared", "summed", "scanned", "flagged", "spread", "picked", "hpicked",
              "horner", "scaled", "stored"]


def rank_program(g, core, T, topo):
    r = T.rank_of(core)
    if r is None:
        return
    S = T.sem
    add, mult, vmax, is_gt = AluOpType.add, AluOpType.mult, AluOpType.max, AluOpType.is_gt
    bound = float(T.tables["BOUND"])
    peers = [T.cores[(r + k) % N] for k in range(1, N)]
    masks = [topo.mask(core, d) for d in peers]
    common = masks[0] & masks[1] & masks[2]
    eng = [bin(m).count("1") for m in masks]
    ceng = bin(common).count("1")
    eng_in = [bin(topo.mask(T.cores[(r - k) % N], core)).count("1") for k in range(1, N)]
    ceng_in = 0
    for k in range(1, N):
        src = T.cores[(r - k) % N]
        m = topo.mask(src, core)
        for j in range(1, N):
            m &= topo.mask(src, T.cores[(r - k + j) % N])
        ceng_in += bin(m).count("1")

    for k in range(1, N):
        b = (r + k) % N
        g.sync.dma_start(T.snd[:, (k - 1) * F:k * F], T.gr[:, b * F:(b + 1) * F]).then_inc(S["ld%d" % k], 16)
    g.sync.dma_start(T.own[:], T.gr[:, r * F:(r + 1) * F]).then_inc(S.ldo, 16)

    for k in range(1, N):
        rid, pid = topo.addr(peers[k - 1], core)
        g.wait_ge(S["ld%d" % k], 16)
        g.remote_dma(T.land[:, (k - 1) * F:k * F], T.snd[:, (k - 1) * F:k * F], S["arr%d" % k], S.sent,
                     pid, rid, masks[k - 1])
    ids = []
    for d in peers:
        rid, pid = topo.addr(d, core)
        ids.append(DstId(rid=rid, pnc=pid))
    g.wait_ge(S.squared, 1)
    g.remote_dma_fused([RemoteDMATransfer(dst_ids=ids, dma_engine_mask=common, remote_sem=S.qarr,
                                          srcs=[T.qall[:, 0:1]],
                                          dsts=[T.qall[:, 3 + k:4 + k] for k in range(1, N)])],
                       local_sem=S.sent)
    g.wait_ge(S.sent, sum(eng) + ceng)

    v = g.vector
    fills = [(T.ones[:], 1.0), (T.qall[:, 1:4], 0.0), (T.cst[:, 0:6], 0.0), (T.cst[:, 6:7], 1.0),
             (T.zer[:], 0.0),
             (T.mul[:, 0:1], 2.0 ** 5), (T.mul[:, 1:NT], 0.25),
             (T.mul[:, NT:2 * NT], 4.0), (T.mul[:, 2 * NT:3 * NT], 2.0),
             (T.fl[:, NT:NS], 0.0), (T.tt[:, NT:NS], -2.0)]
    for j in range(DEG):
        fills.append((T.cf[:, j:j + 1], -POLY[DEG - 1 - j]))
    for ap, val in fills:
        v.memset(ap, val).then_inc(S.fill, 1)
    nfill = len(fills)
    v.wait_ge(S.fill, nfill)
    v.tensor_tensor_scan(T.th[:], T.mul[:, 0:NT], T.zer[:], 2.0 ** (2 * NT - 5), mult, add).then_inc(S.tabs, 1)
    v.tensor_tensor_scan(T.gs[:], T.mul[:, NT:2 * NT], T.zer[:], -(4.0 ** -NT) / 1.5, mult, add).then_inc(S.tabs, 1)
    v.tensor_tensor_scan(T.hn[:], T.mul[:, 2 * NT:3 * NT], T.zer[:], -(2.0 ** -NT), mult, add).then_inc(S.tabs, 1)

    acc = T.acc[:, 0:F]
    v.wait_ge(S.ldo, 16)
    v.wait_ge(S.arr1, eng_in[0])
    v.tensor_tensor(acc, T.own[:], T.land[:, 0:F], add).then_inc(S.added, 1)
    for k in range(2, N):
        v.wait_ge(S["arr%d" % k], eng_in[k - 1])
        v.wait_ge(S.added, k - 1)
        v.tensor_tensor(acc, acc, T.land[:, (k - 1) * F:k * F], add).then_inc(S.added, 1)

    q = T.scn[:, 6:7]
    v.wait_ge(S.added, N - 1)
    v.wait_ge(S.tabs, 3)
    v.wait_ge(S.summed, 1)
    v.tensor_tensor_scan(T.scn[:, 0:7], T.tot[:, 0:7], T.cst[:, 0:7], 0.0, add, vmax).then_inc(S.scanned, 1)
    v.wait_ge(S.scanned, 1)
    v.tensor_scalar(T.fl[:, 0:NT], T.th[:], q, -BIG, is_gt, mult).then_inc(S.flagged, 1)
    v.wait_ge(S.flagged, 1)
    v.wait_ge(S.spread, 1)
    v.tensor_tensor_scan(T.ts[:], T.fl[:], T.tt[:], 0.0, add, vmax).then_inc(S.picked, 1)
    v.tensor_tensor_scan(T.hs[:], T.fl[:, 0:NT], T.hn[:], 0.0, add, vmax).then_inc(S.hpicked, 1)
    v.wait_ge(S.picked, 1)
    v.tensor_tensor_scan(T.ps[:], T.ts[:, NT - 1:NS], T.cf[:], -POLY[DEG], mult, add).then_inc(S.horner, 1)
    v.wait_ge(S.horner, 1)
    v.wait_ge(S.hpicked, 1)
    v.tensor_scalar(T.yo[:], acc, T.hs[:, NT - 1:NT], T.ps[:, DEG - 1:DEG], mult, mult).then_inc(S.scaled, 1)

    a = g.scalar
    a.wait_ge(S.added, N - 1)
    a.activation(T.yo[:], acc, ActivationFunctionType.Square, scale=1.0 / bound,
                 accum_out=T.qall[:, 0:1]).then_inc(S.squared, 1)
    a.wait_ge(S.tabs, 3)
    a.wait_ge(S.scanned, 1)
    a.activation(T.tt[:, 0:NT], T.gs[:], ActivationFunctionType.Identity, bias=5.0 / 3.0, scale=q).then_inc(S.spread, 1)

    p = g.tensor
    p.wait_ge(S.fill, nfill)
    p.wait_ge(S.squared, 1)
    p.wait_ge(S.qarr, ceng_in)
    p.matmul(T.tot[:, 0:7], T.ones[:], T.qall[:, 0:7], True, True).then_inc(S.summed, 1)

    g.sync.wait_ge(S.scaled, 1)
    g.sync.dma_start(T.y[:], T.yo[:]).then_inc(S.stored, 16)
    g.sync.wait_ge(S.stored, 16)
